import numpy as np
import ml_dtypes


def mxq(x, axis, fmt="e4m3"):
    dtype, down = {"e4m3": (ml_dtypes.float8_e4m3fn, 7), "e5m2": (ml_dtypes.float8_e5m2, 14)}[fmt]
    v = np.moveaxis(np.asarray(x, np.float32).astype(ml_dtypes.bfloat16).astype(np.float64), axis, -1)
    blocks = v.reshape(v.shape[:-1] + (-1, 32))
    amax = np.abs(blocks).max(-1, keepdims=True)
    byte = np.maximum(np.where(amax > 0, np.frexp(amax)[1] - 1 + 127, 0) - down, 1)
    scale = np.exp2(byte - 127.0)
    codes = (blocks / scale).astype(np.float32).astype(dtype).astype(np.float64)
    return np.moveaxis((codes * scale).reshape(v.shape), -1, axis)


WIDE = False


def mx_kscale(k):
    if not WIDE:
        return np.ones(k)
    levels = np.array([10, -10, 5, -5, 0])
    if k % 512:
        return np.exp2(np.random.permutation(np.resize(levels, k // 32))).repeat(32)
    a = np.empty((k // 512, 16))
    for p in range(k // 512):
        a[p, :8] = np.random.permutation(np.resize(levels, 8))
        for g in range(8):
            far = levels[np.abs(levels - a[p, g]) >= 10]
            a[p, g + 8] = far[np.random.randint(len(far))]
    return np.exp2(a.ravel()).repeat(32)


def f64(x):
    return np.asarray(x).astype(np.float64)


def striped(idx):
    return np.tile(idx.reshape(-1, 16).T, (8, 1)).astype(np.uint16)


def unstriped(offs):
    return offs[:16].T.reshape(-1).astype(np.int64)


def striped8(idx):
    return np.concatenate([x.reshape(-1, 16).T for x in idx]).astype(np.uint16)


def runs(offs, k):
    lists = np.stack([offs[16 * r : 16 * r + 16].T.reshape(-1) for r in range(8)]).astype(np.int64)
    return lists[np.arange(k) % 512 // 64]


def pack_weight(w):
    k, n = w.shape
    w = f64(np.asarray(w, np.float32).astype(ml_dtypes.bfloat16)).reshape(k // 32, 32, n)
    amax = np.abs(w).max(1)
    byte = np.clip(np.where(amax > 0, np.frexp(amax)[1] - 1 + 127 - 7, 1), 1, 254)
    scaled = (w * np.exp2(127.0 - byte)[:, None, :]).reshape(k, n).astype(np.float32)
    words = np.ascontiguousarray(scaled.reshape(k // 512, 128, 4, n).transpose(0, 1, 3, 2)).astype(ml_dtypes.float8_e4m3fn).view(np.uint8)
    return words, np.ascontiguousarray(byte.astype(np.uint8).reshape(k // 512, 16, n))


def unpack_weight(words, scales):
    g, p, n, _ = words.shape
    vals = np.ascontiguousarray(words).view(ml_dtypes.float8_e4m3fn).astype(np.float64) * np.repeat(np.exp2(scales.astype(np.float64) - 127.0), 8, axis=1)[..., None]
    return vals.transpose(0, 1, 3, 2).reshape(g * 512, n)


def relu(v):
    return np.maximum(v, 0.0)


K, T, S, H, U, C = 512, 2048, 512, 512, 1024, 512


def setup_inputs():
    n = np.random.standard_normal
    s = mx_kscale(K)[:, None]
    packed_xT = pack_weight(n((K, T)) * s)
    return {
        "x_words": packed_xT[0],
        "x_scales": packed_xT[1],
        "w1": (n((K, H)) / np.sqrt(K) / s).astype(np.float32),
        "gs": (np.random.uniform(0.5, 1.5, (K, 1)) / s).astype(np.float32),
        "offs": striped(np.random.permutation(T)[:S]),
        "n1": striped8(np.stack([np.random.permutation(U)[:S] for _ in range(8)])),
        "n2": striped8(np.stack([np.random.permutation(S) for _ in range(8)])),
        "cand": striped(np.random.permutation(T)[:C]),
        "n3": striped8(np.stack([np.random.permutation(U) for _ in range(8)])),
        "n4": striped8(np.stack([np.random.permutation(U) for _ in range(8)])),
    }


def reference(x_words, x_scales, w1, gs, offs, n1, n2, cand, n3, n4):
    x_cand = unpack_weight(x_words, x_scales)[:, unstriped(cand)]
    xq = unpack_weight(x_words, x_scales)[:, unstriped(offs)]
    y = mxq(f64(w1), 0, "e4m3").T @ xq
    nw = y - (relu(y[np.arange(H)[:, None], runs(n2, H)]))
    pg = np.zeros((H, U))
    pg[np.arange(H)[:, None], runs(n1, H)] = nw
    z = f64(gs) * pg
    s = 0.0625 * ((x_cand.T @ mxq(z, 0, "e4m3")))
    sq = (s) ** 2
    return (s[np.arange(C)[:, None], runs(n4, C)]) / (np.sqrt(sq + sq[np.arange(C)[:, None], runs(n3, C)] + 0.25))

@@ -1,0 +1,193 @@
+from contextlib import ExitStack
+
+import concourse.mybir as mybir
+
+K, T, S, H, U, C = 512, 2048, 512, 512, 1024, 512
+FLOPS = 2 * K * H * S + 2 * K * C * U
+
+F32 = mybir.dt.float32
+BF16 = mybir.dt.bfloat16
+I32 = mybir.dt.int32
+U32 = mybir.dt.uint32
+U16 = mybir.dt.uint16
+U8 = mybir.dt.uint8
+FP8X4 = mybir.dt.float8_e4m3fn_x4
+ACT = mybir.ActivationFunctionType
+ALU = mybir.AluOpType
+
+P = 128
+PACK = 4
+BANK = 512
+GROUP = 16
+W_SPLIT = 80
+ORDER = (2, 0, 1, 3)
+
+
+def tile_picked_candpagezrms_none_p_kernel(
+    tc, x_words, x_scales, w1, gs, offs, n1, n2, cand, n3, n4, out
+):
+    nc = tc.nc
+    halves = U // BANK
+
+    with ExitStack() as ctx:
+        lists = ctx.enter_context(tc.tile_pool(name="lists", bufs=1))
+        keep = ctx.enter_context(tc.tile_pool(name="keep", bufs=1))
+        ring = ctx.enter_context(tc.tile_pool(name="ring", bufs=2))
+        psum = ctx.enter_context(tc.psum_pool(name="psum", bufs=8))
+
+        offs_sb = lists.tile([P, S // GROUP], U16, name="offs_sb")
+        cand_sb = lists.tile([P, C // GROUP], U16, name="cand_sb")
+        n1_sb = lists.tile([P, S // GROUP], U16, name="n1_sb")
+        n2_sb = lists.tile([P, S // GROUP], U16, name="n2_sb")
+        n3_sb = lists.tile([P, U // GROUP], U16, name="n3_sb")
+        n4_sb = lists.tile([P, U // GROUP], U16, name="n4_sb")
+
+        table_words = keep.tile([P, T], U32, name="table_words", align_bytes=64)
+        table_scales = keep.tile([P, T], U8, name="table_scales", align_bytes=64)
+        w_raw = keep.tile([P, PACK, H], F32, name="w_raw", align_bytes=64)
+        gs_sb = keep.tile([P, PACK], F32, name="gs_sb")
+
+        nc.vector.memset(table_scales[:].bitcast(I32), 0)
+        nc.sync.dma_start(offs_sb[:], offs)
+        nc.sync.dma_start(cand_sb[:], cand)
+        nc.sync.dma_start(w_raw[:], w1.rearrange("(p j) h -> p j h", j=PACK))
+        nc.sync.dma_start(table_words[:].bitcast(I32), x_words[0].rearrange("p n r -> p (n r)").bitcast(I32))
+        for q in range(4):
+            nc.scalar.dma_start(
+                table_scales[32 * q : 32 * q + 4, :].bitcast(I32), x_scales[0, 4 * q : 4 * q + 4, :].bitcast(I32)
+            )
+        nc.sync.dma_start(n2_sb[:], n2)
+        nc.sync.dma_start(n1_sb[:], n1)
+        nc.sync.dma_start(gs_sb[:], gs.rearrange("(p t) o -> p (t o)", t=PACK))
+        nc.sync.dma_start(n3_sb[:], n3)
+        nc.sync.dma_start(n4_sb[:], n4)
+
+        warm = keep.tile([P, 1], F32, name="warm")
+        warm_out = keep.tile([P, 1], F32, name="warm_out")
+        nc.gpsimd.memset(warm[:], 1.0)
+        nc.scalar.activation(warm_out[:], warm[:], ACT.Abs_reciprocal_sqrt)
+
+        pages = [keep.tile([P, U], F32, name="page%d" % t) for t in range(PACK)]
+        for t in range(PACK):
+            nc.vector.memset(pages[t][:], 0.0)
+
+        tok_scales = keep.tile([P, S], U8, name="tok_scales", align_bytes=64)
+        tok_words = keep.tile([P, S], U32, name="tok_words", align_bytes=64)
+        cand_scales = keep.tile([P, C], U8, name="cand_scales", align_bytes=64)
+        cand_words = keep.tile([P, C], U32, name="cand_words", align_bytes=64)
+        nc.vector.tensor_copy(tok_scales[:], table_scales[:].indirect(offs_sb[:]))
+        nc.vector.tensor_copy(cand_scales[:], table_scales[:].indirect(cand_sb[:]))
+
+        w_bf = keep.tile([P, PACK, P, PACK], BF16, name="w_bf", align_bytes=64)
+        w_src = w_raw[:].rearrange("p j (m t) -> p m j t", t=PACK)
+        w_dst = w_bf[:].rearrange("p t m j -> p m j t")
+        nc.vector.tensor_copy(w_dst[:, :W_SPLIT], w_src[:, :W_SPLIT])
+        nc.scalar.copy(w_dst[:, W_SPLIT:], w_src[:, W_SPLIT:])
+        w_words = keep.tile([P, H], U32, name="w_words", align_bytes=64)
+        w_scales = keep.tile([P, H], U8, name="w_scales", align_bytes=64)
+        nc.vector.quantize_mx(
+            out=w_words[:].bitcast(FP8X4), scales=w_scales[:], in_=w_bf[:].rearrange("p t m j -> p (t m j)")
+        )
+        nc.vector.tensor_copy(tok_words[:], table_words[:].indirect(offs_sb[:]))
+        nc.vector.tensor_copy(cand_words[:], table_words[:].indirect(cand_sb[:]))
+
+        y_pos = [keep.tile([P, S], F32, name="y_pos%d" % t) for t in range(PACK)]
+        y_neg = [keep.tile([P, S], F32, name="y_neg%d" % t)[:] for t in range(PACK - 1)]
+        y_neg.append(pages[ORDER[0]][:, :S])
+        y_acc = {}
+        for t in ORDER:
+            acc = psum.tile([P, BANK], F32, name="acc")
+            cols = slice(t * P, (t + 1) * P)
+            nc.tensor.matmul_mx(
+                out=acc[:],
+                lhsT=w_words[:, cols].bitcast(FP8X4),
+                lhsT_scale=w_scales[:, cols],
+                rhs=tok_words[:].bitcast(FP8X4),
+                rhs_scale=tok_scales[:],
+                start=True,
+                stop=True,
+            )
+            nc.scalar.activation(y_pos[t][:], acc[:], ACT.Relu)
+            y_acc[t] = acc
+            if t != ORDER[-1]:
+                nc.scalar.activation(y_neg[t], acc[:], ACT.Copy, scale=-1.0)
+
+        z_bf = [keep.tile([P, BANK, PACK], BF16, name="z_bf%d" % h, align_bytes=64) for h in range(halves)]
+        fetched = [keep.tile([P, S], F32, name="fetched%d" % t) for t in range(PACK)]
+
+        def fetch(t):
+            for a in range(0, S, S // 2):
+                b = a + S // 2
+                nc.vector.tensor_copy(fetched[t][:, a:b], y_pos[t][:].indirect(n2_sb[:, a // GROUP : b // GROUP]))
+
+        def put(t):
+            nc.vector.tensor_tensor(pages[t][:].indirect(n1_sb[:]), fetched[t][:], y_neg[t], ALU.add)
+            for h in range(halves):
+                src = pages[t][:, h * BANK : (h + 1) * BANK]
+                if t == ORDER[-1] and h == 0:
+                    nc.vector.tensor_scalar_mul(z_bf[h][:, :, t], src, gs_sb[:, t : t + 1])
+                else:
+                    nc.scalar.activation(z_bf[h][:, :, t], src, ACT.Copy, scale=gs_sb[:, t : t + 1])
+
+        dealt_words = keep.tile([P, PACK, P], U32, name="dealt_words", align_bytes=64)
+        dealt_scales = keep.tile([P, PACK, P], U8, name="dealt_scales", align_bytes=64)
+
+        fetch(ORDER[0])
+        for i, t in enumerate(ORDER):
+            if i + 1 < PACK:
+                fetch(ORDER[i + 1])
+            else:
+                nc.vector.tensor_copy(dealt_words[:], cand_words[:].rearrange("p (m t) -> p t m", t=PACK))
+                nc.vector.tensor_copy(
+                    dealt_scales[:].rearrange("p t m -> p m t"), cand_scales[:].rearrange("p (m t) -> p m t", t=PACK)
+                )
+            put(t)
+            if i == 0:
+                nc.scalar.activation(y_neg[ORDER[-1]], y_acc[ORDER[-1]][:], ACT.Copy, scale=-1.0)
+
+        z_words = [keep.tile([P, BANK], U32, name="z_words%d" % h, align_bytes=64) for h in range(halves)]
+        z_scales = [keep.tile([P, BANK], U8, name="z_scales%d" % h, align_bytes=64) for h in range(halves)]
+        for h in range(halves):
+            nc.vector.quantize_mx(
+                out=z_words[h][:].bitcast(FP8X4), scales=z_scales[h][:], in_=z_bf[h][:].rearrange("p w t -> p (w t)")
+            )
+
+        out_rows = out.rearrange("(p t) w -> t p w", t=PACK)
+        for t in range(PACK):
+            score = ring.tile([P, U], F32, name="score")
+            square = ring.tile([P, U], F32, name="square")
+            own = [ring.tile([P, BANK], F32, name="own%d" % h) for h in range(halves)]
+            accs = []
+            for h in range(halves):
+                acc = psum.tile([P, BANK], F32, name="acc")
+                nc.tensor.matmul_mx(
+                    out=acc[:],
+                    lhsT=dealt_words[:, t, :].bitcast(FP8X4),
+                    lhsT_scale=dealt_scales[:, t, :],
+                    rhs=z_words[h][:].bitcast(FP8X4),
+                    rhs_scale=z_scales[h][:],
+                    start=True,
+                    stop=True,
+                )
+                accs.append(acc)
+                nc.scalar.activation(square[:, h * BANK : (h + 1) * BANK], acc[:], ACT.Square, scale=0.0625)
+            for h in range(halves):
+                if t == 0:
+                    nc.vector.tensor_copy(own[h][:], square[:, h * BANK : (h + 1) * BANK])
+                else:
+                    nc.scalar.activation(own[h][:], accs[h][:], ACT.Square, scale=0.0625)
+            for h in range(halves):
+                nc.scalar.activation(score[:, h * BANK : (h + 1) * BANK], accs[h][:], ACT.Copy, scale=-0.0625)
+            roots = []
+            for h in range(halves):
+                entries = slice(h * BANK // GROUP, (h + 1) * BANK // GROUP)
+                total = ring.tile([P, BANK], F32, name="total%d" % h)
+                nc.vector.tensor_tensor(total[:], square[:].indirect(n3_sb[:, entries]), own[h][:], ALU.add)
+                root = ring.tile([P, BANK], F32, name="root%d" % h)
+                nc.scalar.activation(root[:], total[:], ACT.Abs_reciprocal_sqrt, bias=0.25)
+                roots.append(root)
+            for h in range(halves):
+                entries = slice(h * BANK // GROUP, (h + 1) * BANK // GROUP)
+                result = ring.tile([P, BANK], F32, name="result%d" % h)
+                nc.vector.tensor_tensor(result[:], score[:].indirect(n4_sb[:, entries]), roots[h][:], ALU.mult)
+                nc.sync.dma_start(out_rows[t][:, h * BANK : (h + 1) * BANK], result[:])

@@ -19,7 +19,7 @@ P = 128
 PACK = 4
 BANK = 512
 GROUP = 16
-W_SPLIT = 80
+W_SPLIT = 48
 ORDER = (2, 0, 1, 3)
 
 
@@ -47,15 +47,16 @@ def tile_picked_candpagezrms_none_p_kernel(
         w_raw = keep.tile([P, PACK, H], F32, name="w_raw", align_bytes=64)
         gs_sb = keep.tile([P, PACK], F32, name="gs_sb")
 
-        nc.vector.memset(table_scales[:].bitcast(I32), 0)
+        nc.gpsimd.memset(table_scales[:].bitcast(I32), 0)
         nc.sync.dma_start(offs_sb[:], offs)
         nc.sync.dma_start(cand_sb[:], cand)
-        nc.sync.dma_start(w_raw[:], w1.rearrange("(p j) h -> p j h", j=PACK))
-        nc.sync.dma_start(table_words[:].bitcast(I32), x_words[0].rearrange("p n r -> p (n r)").bitcast(I32))
         for q in range(4):
-            nc.scalar.dma_start(
+            queue = nc.sync if q < 2 else nc.scalar
+            queue.dma_start(
                 table_scales[32 * q : 32 * q + 4, :].bitcast(I32), x_scales[0, 4 * q : 4 * q + 4, :].bitcast(I32)
             )
+        nc.sync.dma_start(w_raw[:], w1.rearrange("(p j) h -> p j h", j=PACK))
+        nc.sync.dma_start(table_words[:].bitcast(I32), x_words[0].rearrange("p n r -> p (n r)").bitcast(I32))
         nc.sync.dma_start(n2_sb[:], n2)
         nc.sync.dma_start(n1_sb[:], n1)
         nc.sync.dma_start(gs_sb[:], gs.rearrange("(p t) o -> p (t o)", t=PACK))
@@ -77,6 +78,11 @@ def tile_picked_candpagezrms_none_p_kernel(
         cand_words = keep.tile([P, C], U32, name="cand_words", align_bytes=64)
         nc.vector.tensor_copy(tok_scales[:], table_scales[:].indirect(offs_sb[:]))
         nc.vector.tensor_copy(cand_scales[:], table_scales[:].indirect(cand_sb[:]))
+        dealt_words = keep.tile([P, PACK, P], U32, name="dealt_words", align_bytes=64)
+        dealt_scales = keep.tile([P, PACK, P], U8, name="dealt_scales", align_bytes=64)
+        nc.vector.tensor_copy(
+            dealt_scales[:].rearrange("p t m -> p m t"), cand_scales[:].rearrange("p (m t) -> p m t", t=PACK)
+        )
 
         w_bf = keep.tile([P, PACK, P, PACK], BF16, name="w_bf", align_bytes=64)
         w_src = w_raw[:].rearrange("p j (m t) -> p m j t", t=PACK)
@@ -90,6 +96,7 @@ def tile_picked_candpagezrms_none_p_kernel(
         )
         nc.vector.tensor_copy(tok_words[:], table_words[:].indirect(offs_sb[:]))
         nc.vector.tensor_copy(cand_words[:], table_words[:].indirect(cand_sb[:]))
+        nc.vector.tensor_copy(dealt_words[:], cand_words[:].rearrange("p (m t) -> p t m", t=PACK))
 
         y_pos = [keep.tile([P, S], F32, name="y_pos%d" % t) for t in range(PACK)]
         y_neg = [keep.tile([P, S], F32, name="y_neg%d" % t)[:] for t in range(PACK - 1)]
@@ -129,18 +136,10 @@ def tile_picked_candpagezrms_none_p_kernel(
                 else:
                     nc.scalar.activation(z_bf[h][:, :, t], src, ACT.Copy, scale=gs_sb[:, t : t + 1])
 
-        dealt_words = keep.tile([P, PACK, P], U32, name="dealt_words", align_bytes=64)
-        dealt_scales = keep.tile([P, PACK, P], U8, name="dealt_scales", align_bytes=64)
-
         fetch(ORDER[0])
         for i, t in enumerate(ORDER):
             if i + 1 < PACK:
                 fetch(ORDER[i + 1])
-            else:
-                nc.vector.tensor_copy(dealt_words[:], cand_words[:].rearrange("p (m t) -> p t m", t=PACK))
-                nc.vector.tensor_copy(
-                    dealt_scales[:].rearrange("p t m -> p m t"), cand_scales[:].rearrange("p (m t) -> p m t", t=PACK)
-                )
             put(t)
             if i == 0:
                 nc.scalar.activation(y_neg[ORDER[-1]], y_acc[ORDER[-1]][:], ACT.Copy, scale=-1.0)
@@ -153,15 +152,18 @@ def tile_picked_candpagezrms_none_p_kernel(
             )
 
         out_rows = out.rearrange("(p t) w -> t p w", t=PACK)
-        for t in range(PACK):
-            score = ring.tile([P, U], F32, name="score")
-            square = ring.tile([P, U], F32, name="square")
-            own = [ring.tile([P, BANK], F32, name="own%d" % h) for h in range(halves)]
-            accs = []
+        accs, squares, owns, scores, totals, roots = {}, {}, {}, {}, {}, {}
+
+        def columns(h):
+            return slice(h * BANK, (h + 1) * BANK)
+
+        def multiply(t):
+            squares[t] = ring.tile([P, U], F32, name="square")
+            scores[t] = ring.tile([P, U], F32, name="score")
             for h in range(halves):
-                acc = psum.tile([P, BANK], F32, name="acc")
+                accs[t, h] = psum.tile([P, BANK], F32, name="acc")
                 nc.tensor.matmul_mx(
-                    out=acc[:],
+                    out=accs[t, h][:],
                     lhsT=dealt_words[:, t, :].bitcast(FP8X4),
                     lhsT_scale=dealt_scales[:, t, :],
                     rhs=z_words[h][:].bitcast(FP8X4),
@@ -169,25 +171,55 @@ def tile_picked_candpagezrms_none_p_kernel(
                     start=True,
                     stop=True,
                 )
-                accs.append(acc)
-                nc.scalar.activation(square[:, h * BANK : (h + 1) * BANK], acc[:], ACT.Square, scale=0.0625)
+
+        def square(t, h):
+            nc.scalar.activation(squares[t][:, columns(h)], accs[t, h][:], ACT.Square, scale=0.0625)
+
+        def own_and_score(t):
             for h in range(halves):
-                if t == 0:
-                    nc.vector.tensor_copy(own[h][:], square[:, h * BANK : (h + 1) * BANK])
+                owns[t, h] = ring.tile([P, BANK], F32, name="own%d" % h)
+                if (t, h) == (0, 0):
+                    nc.vector.tensor_copy(owns[t, h][:], squares[t][:, columns(h)])
                 else:
-                    nc.scalar.activation(own[h][:], accs[h][:], ACT.Square, scale=0.0625)
+                    nc.scalar.activation(owns[t, h][:], accs[t, h][:], ACT.Square, scale=0.0625)
             for h in range(halves):
-                nc.scalar.activation(score[:, h * BANK : (h + 1) * BANK], accs[h][:], ACT.Copy, scale=-0.0625)
-            roots = []
+                nc.scalar.activation(scores[t][:, columns(h)], accs[t, h][:], ACT.Copy, scale=-0.0625)
+
+        def root(t, h):
+            entries = slice(h * BANK // GROUP, (h + 1) * BANK // GROUP)
+            total = ring.tile([P, BANK], F32, name="total%d" % h)
+            nc.vector.tensor_tensor(total[:], squares[t][:].indirect(n3_sb[:, entries]), owns[t, h][:], ALU.add)
+            roots[t, h] = ring.tile([P, BANK], F32, name="root%d" % h)
+            nc.scalar.activation(roots[t, h][:], total[:], ACT.Abs_reciprocal_sqrt, bias=0.25)
+
+        def finish(t, h):
+            result = ring.tile([P, BANK], F32, name="result%d" % h)
+            pieces = 2 if (t, h) == (PACK - 1, halves - 1) else 1
+            width = BANK // pieces
+            for a in range(0, BANK, width):
+                first = h * BANK + a
+                entries = slice(first // GROUP, (first + width) // GROUP)
+                nc.vector.tensor_tensor(
+                    result[:, a : a + width],
+                    scores[t][:].indirect(n4_sb[:, entries]),
+                    roots[t, h][:, a : a + width],
+                    ALU.mult,
+                )
+                nc.sync.dma_start(out_rows[t][:, first : first + width], result[:, a : a + width])
+
+        multiply(0)
+        for h in range(halves):
+            square(0, h)
+        own_and_score(0)
+        for t in range(PACK):
+            more = t + 1 < PACK
+            if more:
+                multiply(t + 1)
             for h in range(halves):
-                entries = slice(h * BANK // GROUP, (h + 1) * BANK // GROUP)
-                total = ring.tile([P, BANK], F32, name="total%d" % h)
-                nc.vector.tensor_tensor(total[:], square[:].indirect(n3_sb[:, entries]), own[h][:], ALU.add)
-                root = ring.tile([P, BANK], F32, name="root%d" % h)
-                nc.scalar.activation(root[:], total[:], ACT.Abs_reciprocal_sqrt, bias=0.25)
-                roots.append(root)
+                root(t, h)
+                if more:
+                    square(t + 1, h)
             for h in range(halves):
-                entries = slice(h * BANK // GROUP, (h + 1) * BANK // GROUP)
-                result = ring.tile([P, BANK], F32, name="result%d" % h)
-                nc.vector.tensor_tensor(result[:], score[:].indirect(n4_sb[:, entries]), roots[h][:], ALU.mult)
-                nc.sync.dma_start(out_rows[t][:, h * BANK : (h + 1) * BANK], result[:])
+                finish(t, h)
+            if more:
+                own_and_score(t + 1)

@@ -19,6 +19,7 @@ P = 128
 PACK = 4
 BANK = 512
 GROUP = 16
+CHUNK = 256
 W_SPLIT = 48
 ORDER = (2, 0, 1, 3)
 
@@ -28,6 +29,7 @@ def tile_picked_candpagezrms_none_p_kernel(
 ):
     nc = tc.nc
     halves = U // BANK
+    chunks = U // CHUNK
 
     with ExitStack() as ctx:
         lists = ctx.enter_context(tc.tile_pool(name="lists", bufs=1))
@@ -78,7 +80,6 @@ def tile_picked_candpagezrms_none_p_kernel(
         cand_words = keep.tile([P, C], U32, name="cand_words", align_bytes=64)
         nc.vector.tensor_copy(tok_scales[:], table_scales[:].indirect(offs_sb[:]))
         nc.vector.tensor_copy(cand_scales[:], table_scales[:].indirect(cand_sb[:]))
-        dealt_words = keep.tile([P, PACK, P], U32, name="dealt_words", align_bytes=64)
         dealt_scales = keep.tile([P, PACK, P], U8, name="dealt_scales", align_bytes=64)
         nc.vector.tensor_copy(
             dealt_scales[:].rearrange("p t m -> p m t"), cand_scales[:].rearrange("p (m t) -> p m t", t=PACK)
@@ -96,7 +97,6 @@ def tile_picked_candpagezrms_none_p_kernel(
         )
         nc.vector.tensor_copy(tok_words[:], table_words[:].indirect(offs_sb[:]))
         nc.vector.tensor_copy(cand_words[:], table_words[:].indirect(cand_sb[:]))
-        nc.vector.tensor_copy(dealt_words[:], cand_words[:].rearrange("p (m t) -> p t m", t=PACK))
 
         y_pos = [keep.tile([P, S], F32, name="y_pos%d" % t) for t in range(PACK)]
         y_neg = [keep.tile([P, S], F32, name="y_neg%d" % t)[:] for t in range(PACK - 1)]
@@ -119,8 +119,8 @@ def tile_picked_candpagezrms_none_p_kernel(
             if t != ORDER[-1]:
                 nc.scalar.activation(y_neg[t], acc[:], ACT.Copy, scale=-1.0)
 
-        z_bf = [keep.tile([P, BANK, PACK], BF16, name="z_bf%d" % h, align_bytes=64) for h in range(halves)]
-        fetched = [keep.tile([P, S], F32, name="fetched%d" % t) for t in range(PACK)]
+        z_bf = [keep.tile([P, CHUNK, PACK], BF16, name="z_bf%d" % c, align_bytes=64) for c in range(chunks)]
+        fetched = [keep.tile([P, S], F32, name="fetched%d" % t, align_bytes=64) for t in range(PACK)]
 
         def fetch(t):
             for a in range(0, S, S // 2):
@@ -129,26 +129,32 @@ def tile_picked_candpagezrms_none_p_kernel(
 
         def put(t):
             nc.vector.tensor_tensor(pages[t][:].indirect(n1_sb[:]), fetched[t][:], y_neg[t], ALU.add)
-            for h in range(halves):
-                src = pages[t][:, h * BANK : (h + 1) * BANK]
-                if t == ORDER[-1] and h == 0:
-                    nc.vector.tensor_scalar_mul(z_bf[h][:, :, t], src, gs_sb[:, t : t + 1])
+            for c in range(chunks):
+                src = pages[t][:, c * CHUNK : (c + 1) * CHUNK]
+                if t == ORDER[-1] and c < chunks // 2:
+                    nc.vector.tensor_scalar_mul(z_bf[c][:, :, t], src, gs_sb[:, t : t + 1])
                 else:
-                    nc.scalar.activation(z_bf[h][:, :, t], src, ACT.Copy, scale=gs_sb[:, t : t + 1])
+                    nc.scalar.activation(z_bf[c][:, :, t], src, ACT.Copy, scale=gs_sb[:, t : t + 1])
 
         fetch(ORDER[0])
         for i, t in enumerate(ORDER):
             if i + 1 < PACK:
                 fetch(ORDER[i + 1])
+            else:
+                dealt_words = keep.tile([P, PACK, P], U32, name="fetched%d" % ORDER[-2], align_bytes=64)
+                nc.vector.tensor_copy(dealt_words[:], cand_words[:].rearrange("p (m t) -> p t m", t=PACK))
             put(t)
             if i == 0:
                 nc.scalar.activation(y_neg[ORDER[-1]], y_acc[ORDER[-1]][:], ACT.Copy, scale=-1.0)
 
         z_words = [keep.tile([P, BANK], U32, name="z_words%d" % h, align_bytes=64) for h in range(halves)]
         z_scales = [keep.tile([P, BANK], U8, name="z_scales%d" % h, align_bytes=64) for h in range(halves)]
-        for h in range(halves):
+        for c in range(chunks):
+            h, a = divmod(c * CHUNK, BANK)
             nc.vector.quantize_mx(
-                out=z_words[h][:].bitcast(FP8X4), scales=z_scales[h][:], in_=z_bf[h][:].rearrange("p w t -> p (w t)")
+                out=z_words[h][:, a : a + CHUNK].bitcast(FP8X4),
+                scales=z_scales[h][:, a : a + CHUNK],
+                in_=z_bf[c][:].rearrange("p w t -> p (w t)"),
             )
 
         out_rows = out.rearrange("(p t) w -> t p w", t=PACK)
@@ -160,20 +166,28 @@ def tile_picked_candpagezrms_none_p_kernel(
         def multiply(t):
             squares[t] = ring.tile([P, U], F32, name="square")
             scores[t] = ring.tile([P, U], F32, name="score")
+            width = CHUNK if t == 0 else BANK
             for h in range(halves):
-                accs[t, h] = psum.tile([P, BANK], F32, name="acc")
-                nc.tensor.matmul_mx(
-                    out=accs[t, h][:],
-                    lhsT=dealt_words[:, t, :].bitcast(FP8X4),
-                    lhsT_scale=dealt_scales[:, t, :],
-                    rhs=z_words[h][:].bitcast(FP8X4),
-                    rhs_scale=z_scales[h][:],
-                    start=True,
-                    stop=True,
-                )
+                accs[t, h] = []
+                for a in range(0, BANK, width):
+                    acc = psum.tile([P, width], F32, name="acc")
+                    nc.tensor.matmul_mx(
+                        out=acc[:],
+                        lhsT=dealt_words[:, t, :].bitcast(FP8X4),
+                        lhsT_scale=dealt_scales[:, t, :],
+                        rhs=z_words[h][:, a : a + width].bitcast(FP8X4),
+                        rhs_scale=z_scales[h][:, a : a + width],
+                        start=True,
+                        stop=True,
+                    )
+                    accs[t, h].append((acc, slice(a, a + width)))
+
+        def empty(t, h, target, func, scale):
+            for acc, part in accs[t, h]:
+                nc.scalar.activation(target[:, part], acc[:], func, scale=scale)
 
         def square(t, h):
-            nc.scalar.activation(squares[t][:, columns(h)], accs[t, h][:], ACT.Square, scale=0.0625)
+            empty(t, h, squares[t][:, columns(h)], ACT.Square, 0.0625)
 
         def own_and_score(t):
             for h in range(halves):
@@ -181,9 +195,9 @@ def tile_picked_candpagezrms_none_p_kernel(
                 if (t, h) == (0, 0):
                     nc.vector.tensor_copy(owns[t, h][:], squares[t][:, columns(h)])
                 else:
-                    nc.scalar.activation(owns[t, h][:], accs[t, h][:], ACT.Square, scale=0.0625)
+                    empty(t, h, owns[t, h][:], ACT.Square, 0.0625)
             for h in range(halves):
-                nc.scalar.activation(scores[t][:, columns(h)], accs[t, h][:], ACT.Copy, scale=-0.0625)
+                empty(t, h, scores[t][:, columns(h)], ACT.Copy, -0.0625)
 
         def root(t, h):
             entries = slice(h * BANK // GROUP, (h + 1) * BANK // GROUP)

@@ -17,11 +17,16 @@ ALU = mybir.AluOpType
 
 P = 128
 PACK = 4
+QUADRANT = 32
 BANK = 512
 GROUP = 16
 CHUNK = 256
 W_SPLIT = 48
 ORDER = (2, 0, 1, 3)
+
+
+def entries(first, count):
+    return slice(first // GROUP, (first + count) // GROUP)
 
 
 def tile_picked_candpagezrms_none_p_kernel(
@@ -30,6 +35,7 @@ def tile_picked_candpagezrms_none_p_kernel(
     nc = tc.nc
     halves = U // BANK
     chunks = U // CHUNK
+    first_plane, last_plane = ORDER[0], ORDER[-1]
 
     with ExitStack() as ctx:
         lists = ctx.enter_context(tc.tile_pool(name="lists", bufs=1))
@@ -52,10 +58,11 @@ def tile_picked_candpagezrms_none_p_kernel(
         nc.gpsimd.memset(table_scales[:].bitcast(I32), 0)
         nc.sync.dma_start(offs_sb[:], offs)
         nc.sync.dma_start(cand_sb[:], cand)
-        for q in range(4):
+        for q in range(P // QUADRANT):
             queue = nc.sync if q < 2 else nc.scalar
             queue.dma_start(
-                table_scales[32 * q : 32 * q + 4, :].bitcast(I32), x_scales[0, 4 * q : 4 * q + 4, :].bitcast(I32)
+                table_scales[QUADRANT * q : QUADRANT * q + 4, :].bitcast(I32),
+                x_scales[0, 4 * q : 4 * q + 4, :].bitcast(I32),
             )
         nc.sync.dma_start(w_raw[:], w1.rearrange("(p j) h -> p j h", j=PACK))
         nc.sync.dma_start(table_words[:].bitcast(I32), x_words[0].rearrange("p n r -> p (n r)").bitcast(I32))
@@ -95,57 +102,55 @@ def tile_picked_candpagezrms_none_p_kernel(
         nc.vector.quantize_mx(
             out=w_words[:].bitcast(FP8X4), scales=w_scales[:], in_=w_bf[:].rearrange("p t m j -> p (t m j)")
         )
-        nc.vector.tensor_copy(tok_words[:], table_words[:].indirect(offs_sb[:]))
+        for a in range(0, S, CHUNK):
+            nc.vector.tensor_copy(tok_words[:, a : a + CHUNK], table_words[:].indirect(offs_sb[:, entries(a, CHUNK)]))
         nc.vector.tensor_copy(cand_words[:], table_words[:].indirect(cand_sb[:]))
 
-        y_pos = [keep.tile([P, S], F32, name="y_pos%d" % t) for t in range(PACK)]
-        y_neg = [keep.tile([P, S], F32, name="y_neg%d" % t)[:] for t in range(PACK - 1)]
-        y_neg.append(pages[ORDER[0]][:, :S])
-        y_acc = {}
+        y_both = [keep.tile([P, 2 * S], F32, name="y_both%d" % t) for t in range(PACK)]
         for t in ORDER:
-            acc = psum.tile([P, BANK], F32, name="acc")
             cols = slice(t * P, (t + 1) * P)
-            nc.tensor.matmul_mx(
-                out=acc[:],
-                lhsT=w_words[:, cols].bitcast(FP8X4),
-                lhsT_scale=w_scales[:, cols],
-                rhs=tok_words[:].bitcast(FP8X4),
-                rhs_scale=tok_scales[:],
-                start=True,
-                stop=True,
-            )
-            nc.scalar.activation(y_pos[t][:], acc[:], ACT.Relu)
-            y_acc[t] = acc
-            if t != ORDER[-1]:
-                nc.scalar.activation(y_neg[t], acc[:], ACT.Copy, scale=-1.0)
+            width = CHUNK if t == first_plane else S
+            for a in range(0, S, width):
+                acc = psum.tile([P, width], F32, name="acc")
+                nc.tensor.matmul_mx(
+                    out=acc[:],
+                    lhsT=w_words[:, cols].bitcast(FP8X4),
+                    lhsT_scale=w_scales[:, cols],
+                    rhs=tok_words[:, a : a + width].bitcast(FP8X4),
+                    rhs_scale=tok_scales[:, a : a + width],
+                    start=True,
+                    stop=True,
+                )
+                nc.scalar.activation(y_both[t][:, a : a + width], acc[:], ACT.Relu)
+                nc.scalar.activation(y_both[t][:, S + a : S + a + width], acc[:], ACT.Copy, scale=-1.0)
 
         z_bf = [keep.tile([P, CHUNK, PACK], BF16, name="z_bf%d" % c, align_bytes=64) for c in range(chunks)]
         fetched = [keep.tile([P, S], F32, name="fetched%d" % t, align_bytes=64) for t in range(PACK)]
+        last_gs = [pages[first_plane][:, c * CHUNK : c * CHUNK + 1] for c in range(chunks // 2)]
 
         def fetch(t):
-            for a in range(0, S, S // 2):
-                b = a + S // 2
-                nc.vector.tensor_copy(fetched[t][:, a:b], y_pos[t][:].indirect(n2_sb[:, a // GROUP : b // GROUP]))
+            nc.vector.tensor_copy(fetched[t][:], y_both[t][:].indirect(n2_sb[:]))
 
         def put(t):
-            nc.vector.tensor_tensor(pages[t][:].indirect(n1_sb[:]), fetched[t][:], y_neg[t], ALU.add)
+            nc.vector.tensor_tensor(pages[t][:].indirect(n1_sb[:]), fetched[t][:], y_both[t][:, S:], ALU.add)
             for c in range(chunks):
                 src = pages[t][:, c * CHUNK : (c + 1) * CHUNK]
-                if t == ORDER[-1] and c < chunks // 2:
-                    nc.vector.tensor_scalar_mul(z_bf[c][:, :, t], src, gs_sb[:, t : t + 1])
+                if t == last_plane and c < len(last_gs):
+                    nc.vector.tensor_scalar_mul(z_bf[c][:, :, t], src, last_gs[c])
                 else:
                     nc.scalar.activation(z_bf[c][:, :, t], src, ACT.Copy, scale=gs_sb[:, t : t + 1])
 
-        fetch(ORDER[0])
+        fetch(first_plane)
         for i, t in enumerate(ORDER):
-            if i + 1 < PACK:
+            if t != last_plane:
                 fetch(ORDER[i + 1])
             else:
-                dealt_words = keep.tile([P, PACK, P], U32, name="fetched%d" % ORDER[-2], align_bytes=64)
+                dealt_words = keep.tile([P, PACK, P], U32, name="fetched%d" % ORDER[i - 1], align_bytes=64)
                 nc.vector.tensor_copy(dealt_words[:], cand_words[:].rearrange("p (m t) -> p t m", t=PACK))
             put(t)
-            if i == 0:
-                nc.scalar.activation(y_neg[ORDER[-1]], y_acc[ORDER[-1]][:], ACT.Copy, scale=-1.0)
+            if t == first_plane:
+                for column in last_gs:
+                    nc.scalar.copy(column, gs_sb[:, last_plane : last_plane + 1])
 
         z_words = [keep.tile([P, BANK], U32, name="z_words%d" % h, align_bytes=64) for h in range(halves)]
         z_scales = [keep.tile([P, BANK], U8, name="z_scales%d" % h, align_bytes=64) for h in range(halves)]
@@ -158,7 +163,7 @@ def tile_picked_candpagezrms_none_p_kernel(
             )
 
         out_rows = out.rearrange("(p t) w -> t p w", t=PACK)
-        accs, squares, owns, scores, totals, roots = {}, {}, {}, {}, {}, {}
+        accs, squares, owns, scores, roots = {}, {}, {}, {}, {}
 
         def columns(h):
             return slice(h * BANK, (h + 1) * BANK)
@@ -200,26 +205,24 @@ def tile_picked_candpagezrms_none_p_kernel(
                 empty(t, h, scores[t][:, columns(h)], ACT.Copy, -0.0625)
 
         def root(t, h):
-            entries = slice(h * BANK // GROUP, (h + 1) * BANK // GROUP)
             total = ring.tile([P, BANK], F32, name="total%d" % h)
-            nc.vector.tensor_tensor(total[:], squares[t][:].indirect(n3_sb[:, entries]), owns[t, h][:], ALU.add)
+            looked_up = squares[t][:].indirect(n3_sb[:, entries(h * BANK, BANK)])
+            nc.vector.tensor_tensor(total[:], looked_up, owns[t, h][:], ALU.add)
             roots[t, h] = ring.tile([P, BANK], F32, name="root%d" % h)
             nc.scalar.activation(roots[t, h][:], total[:], ACT.Abs_reciprocal_sqrt, bias=0.25)
 
         def finish(t, h):
             result = ring.tile([P, BANK], F32, name="result%d" % h)
-            pieces = 2 if (t, h) == (PACK - 1, halves - 1) else 1
-            width = BANK // pieces
+            width = CHUNK if (t, h) == (PACK - 1, halves - 1) else BANK
             for a in range(0, BANK, width):
-                first = h * BANK + a
-                entries = slice(first // GROUP, (first + width) // GROUP)
+                slot = h * BANK + a
                 nc.vector.tensor_tensor(
                     result[:, a : a + width],
-                    scores[t][:].indirect(n4_sb[:, entries]),
+                    scores[t][:].indirect(n4_sb[:, entries(slot, width)]),
                     roots[t, h][:, a : a + width],
                     ALU.mult,
                 )
-                nc.sync.dma_start(out_rows[t][:, first : first + width], result[:, a : a + width])
+                nc.sync.dma_start(out_rows[t][:, slot : slot + width], result[:, a : a + width])
 
         multiply(0)
         for h in range(halves):

from contextlib import ExitStack

import concourse.mybir as mybir

K, T, S, H, U, C = 512, 2048, 512, 512, 1024, 512
FLOPS = 2 * K * H * S + 2 * K * C * U

F32 = mybir.dt.float32
BF16 = mybir.dt.bfloat16
I32 = mybir.dt.int32
U32 = mybir.dt.uint32
U16 = mybir.dt.uint16
U8 = mybir.dt.uint8
FP8X4 = mybir.dt.float8_e4m3fn_x4
ACT = mybir.ActivationFunctionType
ALU = mybir.AluOpType

P = 128
PACK = 4
QUADRANT = 32
BANK = 512
GROUP = 16
CHUNK = 256
W_SPLIT = 48
ORDER = (2, 0, 1, 3)


def entries(first, count):
    return slice(first // GROUP, (first + count) // GROUP)


def tile_picked_candpagezrms_none_p_kernel(
    tc, x_words, x_scales, w1, gs, offs, n1, n2, cand, n3, n4, out
):
    nc = tc.nc
    halves = U // BANK
    chunks = U // CHUNK
    first_plane, last_plane = ORDER[0], ORDER[-1]

    with ExitStack() as ctx:
        lists = ctx.enter_context(tc.tile_pool(name="lists", bufs=1))
        keep = ctx.enter_context(tc.tile_pool(name="keep", bufs=1))
        ring = ctx.enter_context(tc.tile_pool(name="ring", bufs=2))
        psum = ctx.enter_context(tc.psum_pool(name="psum", bufs=8))

        offs_sb = lists.tile([P, S // GROUP], U16, name="offs_sb")
        cand_sb = lists.tile([P, C // GROUP], U16, name="cand_sb")
        n1_sb = lists.tile([P, S // GROUP], U16, name="n1_sb")
        n2_sb = lists.tile([P, S // GROUP], U16, name="n2_sb")
        n3_sb = lists.tile([P, U // GROUP], U16, name="n3_sb")
        n4_sb = lists.tile([P, U // GROUP], U16, name="n4_sb")

        table_words = keep.tile([P, T], U32, name="table_words", align_bytes=64)
        table_scales = keep.tile([P, T], U8, name="table_scales", align_bytes=64)
        w_raw = keep.tile([P, PACK, H], F32, name="w_raw", align_bytes=64)
        gs_sb = keep.tile([P, PACK], F32, name="gs_sb")

        nc.gpsimd.memset(table_scales[:].bitcast(I32), 0)
        nc.sync.dma_start(offs_sb[:], offs)
        nc.sync.dma_start(cand_sb[:], cand)
        for q in range(P // QUADRANT):
            queue = nc.sync if q < 2 else nc.scalar
            queue.dma_start(
                table_scales[QUADRANT * q : QUADRANT * q + 4, :].bitcast(I32),
                x_scales[0, 4 * q : 4 * q + 4, :].bitcast(I32),
            )
        nc.sync.dma_start(w_raw[:], w1.rearrange("(p j) h -> p j h", j=PACK))
        nc.sync.dma_start(table_words[:].bitcast(I32), x_words[0].rearrange("p n r -> p (n r)").bitcast(I32))
        nc.sync.dma_start(n2_sb[:], n2)
        nc.sync.dma_start(n1_sb[:], n1)
        nc.sync.dma_start(gs_sb[:], gs.rearrange("(p t) o -> p (t o)", t=PACK))
        nc.sync.dma_start(n3_sb[:], n3)
        nc.sync.dma_start(n4_sb[:], n4)

        warm = keep.tile([P, 1], F32, name="warm")
        warm_out = keep.tile([P, 1], F32, name="warm_out")
        nc.gpsimd.memset(warm[:], 1.0)
        nc.scalar.activation(warm_out[:], warm[:], ACT.Abs_reciprocal_sqrt)

        pages = [keep.tile([P, U], F32, name="page%d" % t) for t in range(PACK)]
        for t in range(PACK):
            nc.vector.memset(pages[t][:], 0.0)

        tok_scales = keep.tile([P, S], U8, name="tok_scales", align_bytes=64)
        tok_words = keep.tile([P, S], U32, name="tok_words", align_bytes=64)
        cand_scales = keep.tile([P, C], U8, name="cand_scales", align_bytes=64)
        cand_words = keep.tile([P, C], U32, name="cand_words", align_bytes=64)
        nc.vector.tensor_copy(tok_scales[:], table_scales[:].indirect(offs_sb[:]))
        nc.vector.tensor_copy(cand_scales[:], table_scales[:].indirect(cand_sb[:]))
        dealt_scales = keep.tile([P, PACK, P], U8, name="dealt_scales", align_bytes=64)
        nc.vector.tensor_copy(
            dealt_scales[:].rearrange("p t m -> p m t"), cand_scales[:].rearrange("p (m t) -> p m t", t=PACK)
        )

        w_bf = keep.tile([P, PACK, P, PACK], BF16, name="w_bf", align_bytes=64)
        w_src = w_raw[:].rearrange("p j (m t) -> p m j t", t=PACK)
        w_dst = w_bf[:].rearrange("p t m j -> p m j t")
        nc.vector.tensor_copy(w_dst[:, :W_SPLIT], w_src[:, :W_SPLIT])
        nc.scalar.copy(w_dst[:, W_SPLIT:], w_src[:, W_SPLIT:])
        w_words = keep.tile([P, H], U32, name="w_words", align_bytes=64)
        w_scales = keep.tile([P, H], U8, name="w_scales", align_bytes=64)
        nc.vector.quantize_mx(
            out=w_words[:].bitcast(FP8X4), scales=w_scales[:], in_=w_bf[:].rearrange("p t m j -> p (t m j)")
        )
        for a in range(0, S, CHUNK):
            nc.vector.tensor_copy(tok_words[:, a : a + CHUNK], table_words[:].indirect(offs_sb[:, entries(a, CHUNK)]))
        nc.vector.tensor_copy(cand_words[:], table_words[:].indirect(cand_sb[:]))

        y_both = [keep.tile([P, 2 * S], F32, name="y_both%d" % t) for t in range(PACK)]
        for t in ORDER:
            cols = slice(t * P, (t + 1) * P)
            width = CHUNK if t == first_plane else S
            for a in range(0, S, width):
                acc = psum.tile([P, width], F32, name="acc")
                nc.tensor.matmul_mx(
                    out=acc[:],
                    lhsT=w_words[:, cols].bitcast(FP8X4),
                    lhsT_scale=w_scales[:, cols],
                    rhs=tok_words[:, a : a + width].bitcast(FP8X4),
                    rhs_scale=tok_scales[:, a : a + width],
                    start=True,
                    stop=True,
                )
                nc.scalar.activation(y_both[t][:, a : a + width], acc[:], ACT.Relu)
                nc.scalar.activation(y_both[t][:, S + a : S + a + width], acc[:], ACT.Copy, scale=-1.0)

        z_bf = [keep.tile([P, CHUNK, PACK], BF16, name="z_bf%d" % c, align_bytes=64) for c in range(chunks)]
        fetched = [keep.tile([P, S], F32, name="fetched%d" % t, align_bytes=64) for t in range(PACK)]
        last_gs = [pages[first_plane][:, c * CHUNK : c * CHUNK + 1] for c in range(chunks // 2)]

        def fetch(t):
            nc.vector.tensor_copy(fetched[t][:], y_both[t][:].indirect(n2_sb[:]))

        def put(t):
            nc.vector.tensor_tensor(pages[t][:].indirect(n1_sb[:]), fetched[t][:], y_both[t][:, S:], ALU.add)
            for c in range(chunks):
                src = pages[t][:, c * CHUNK : (c + 1) * CHUNK]
                if t == last_plane and c < len(last_gs):
                    nc.vector.tensor_scalar_mul(z_bf[c][:, :, t], src, last_gs[c])
                else:
                    nc.scalar.activation(z_bf[c][:, :, t], src, ACT.Copy, scale=gs_sb[:, t : t + 1])

        fetch(first_plane)
        for i, t in enumerate(ORDER):
            if t != last_plane:
                fetch(ORDER[i + 1])
            else:
                dealt_words = keep.tile([P, PACK, P], U32, name="fetched%d" % ORDER[i - 1], align_bytes=64)
                nc.vector.tensor_copy(dealt_words[:], cand_words[:].rearrange("p (m t) -> p t m", t=PACK))
            put(t)
            if t == first_plane:
                for column in last_gs:
                    nc.scalar.copy(column, gs_sb[:, last_plane : last_plane + 1])

        z_words = [keep.tile([P, BANK], U32, name="z_words%d" % h, align_bytes=64) for h in range(halves)]
        z_scales = [keep.tile([P, BANK], U8, name="z_scales%d" % h, align_bytes=64) for h in range(halves)]
        for c in range(chunks):
            h, a = divmod(c * CHUNK, BANK)
            nc.vector.quantize_mx(
                out=z_words[h][:, a : a + CHUNK].bitcast(FP8X4),
                scales=z_scales[h][:, a : a + CHUNK],
                in_=z_bf[c][:].rearrange("p w t -> p (w t)"),
            )

        out_rows = out.rearrange("(p t) w -> t p w", t=PACK)
        accs, squares, owns, scores, roots = {}, {}, {}, {}, {}

        def columns(h):
            return slice(h * BANK, (h + 1) * BANK)

        def multiply(t):
            squares[t] = ring.tile([P, U], F32, name="square")
            scores[t] = ring.tile([P, U], F32, name="score")
            width = CHUNK if t == 0 else BANK
            for h in range(halves):
                accs[t, h] = []
                for a in range(0, BANK, width):
                    acc = psum.tile([P, width], F32, name="acc")
                    nc.tensor.matmul_mx(
                        out=acc[:],
                        lhsT=dealt_words[:, t, :].bitcast(FP8X4),
                        lhsT_scale=dealt_scales[:, t, :],
                        rhs=z_words[h][:, a : a + width].bitcast(FP8X4),
                        rhs_scale=z_scales[h][:, a : a + width],
                        start=True,
                        stop=True,
                    )
                    accs[t, h].append((acc, slice(a, a + width)))

        def empty(t, h, target, func, scale):
            for acc, part in accs[t, h]:
                nc.scalar.activation(target[:, part], acc[:], func, scale=scale)

        def square(t, h):
            empty(t, h, squares[t][:, columns(h)], ACT.Square, 0.0625)

        def own_and_score(t):
            for h in range(halves):
                owns[t, h] = ring.tile([P, BANK], F32, name="own%d" % h)
                if (t, h) == (0, 0):
                    nc.vector.tensor_copy(owns[t, h][:], squares[t][:, columns(h)])
                else:
                    empty(t, h, owns[t, h][:], ACT.Square, 0.0625)
            for h in range(halves):
                empty(t, h, scores[t][:, columns(h)], ACT.Copy, -0.0625)

        def root(t, h):
            total = ring.tile([P, BANK], F32, name="total%d" % h)
            looked_up = squares[t][:].indirect(n3_sb[:, entries(h * BANK, BANK)])
            nc.vector.tensor_tensor(total[:], looked_up, owns[t, h][:], ALU.add)
            roots[t, h] = ring.tile([P, BANK], F32, name="root%d" % h)
            nc.scalar.activation(roots[t, h][:], total[:], ACT.Abs_reciprocal_sqrt, bias=0.25)

        def finish(t, h):
            result = ring.tile([P, BANK], F32, name="result%d" % h)
            width = CHUNK if (t, h) == (PACK - 1, halves - 1) else BANK
            for a in range(0, BANK, width):
                slot = h * BANK + a
                nc.vector.tensor_tensor(
                    result[:, a : a + width],
                    scores[t][:].indirect(n4_sb[:, entries(slot, width)]),
                    roots[t, h][:, a : a + width],
                    ALU.mult,
                )
                nc.sync.dma_start(out_rows[t][:, slot : slot + width], result[:, a : a + width])

        multiply(0)
        for h in range(halves):
            square(0, h)
        own_and_score(0)
        for t in range(PACK):
            more = t + 1 < PACK
            if more:
                multiply(t + 1)
            for h in range(halves):
                root(t, h)
                if more:
                    square(t + 1, h)
            for h in range(halves):
                finish(t, h)
            if more:
                own_and_score(t + 1)
